import numpy as np
import ml_dtypes


def mxq(x, axis, fmt="e4m3"):
    dtype, down = {"e4m3": (ml_dtypes.float8_e4m3fn, 7), "e5m2": (ml_dtypes.float8_e5m2, 14)}[fmt]
    v = np.moveaxis(np.asarray(x, np.float32).astype(ml_dtypes.bfloat16).astype(np.float64), axis, -1)
    blocks = v.reshape(v.shape[:-1] + (-1, 32))
    amax = np.abs(blocks).max(-1, keepdims=True)
    byte = np.maximum(np.where(amax > 0, np.frexp(amax)[1] - 1 + 127, 0) - down, 1)
    scale = np.exp2(byte - 127.0)
    codes = (blocks / scale).astype(np.float32).astype(dtype).astype(np.float64)
    return np.moveaxis((codes * scale).reshape(v.shape), -1, axis)


WIDE = False


def mx_kscale(k):
    if not WIDE:
        return np.ones(k)
    levels = np.array([10, -10, 5, -5, 0])
    if k % 512:
        return np.exp2(np.random.permutation(np.resize(levels, k // 32))).repeat(32)
    a = np.empty((k // 512, 16))
    for p in range(k // 512):
        a[p, :8] = np.random.permutation(np.resize(levels, 8))
        for g in range(8):
            far = levels[np.abs(levels - a[p, g]) >= 10]
            a[p, g + 8] = far[np.random.randint(len(far))]
    return np.exp2(a.ravel()).repeat(32)


BF16 = ml_dtypes.bfloat16


def bf(x):
    return np.asarray(x, np.float32).astype(BF16)


def f64(x):
    return np.asarray(x).astype(np.float64)


E2M1 = np.array([0.0, 0.5, 1.0, 1.5, 2.0, 3.0, 4.0, 6.0, -0.0, -0.5, -1.0, -1.5, -2.0, -3.0, -4.0, -6.0])


def pack_weight(w, fmt):
    k, n = w.shape
    w = f64(bf(w)).reshape(k // 32, 32, n)
    amax = np.abs(w).max(1)
    if fmt == "e4m3":
        byte = np.frexp(amax)[1] - 1 + 127 - 7
    else:
        mant, ex = np.frexp(amax / 6.0)
        byte = np.where(mant > 0.5, ex, ex - 1) + 127
    byte = np.clip(np.where(amax > 0, byte, 1), 1, 254)
    scaled = (w * np.exp2(127.0 - byte)[:, None, :]).reshape(k, n).astype(np.float32)
    by_word = np.ascontiguousarray(scaled.reshape(k // 512, 128, 4, n).transpose(0, 1, 3, 2))
    if fmt == "e4m3":
        words = by_word.astype(ml_dtypes.float8_e4m3fn).view(np.uint8)
    else:
        c = by_word.astype(ml_dtypes.float4_e2m1fn).view(np.uint8) & 0xF
        words = c[..., 0::2] | (c[..., 1::2] << 4)
    return np.ascontiguousarray(words), np.ascontiguousarray(byte.astype(np.uint8).reshape(k // 512, 16, n))


def unpack_weight(words, scales, fmt):
    g, p, n, _ = words.shape
    if fmt == "e4m3":
        vals = np.ascontiguousarray(words).view(ml_dtypes.float8_e4m3fn).astype(np.float64)
    else:
        nib = np.empty((g, p, n, 4), np.uint8)
        nib[..., 0::2] = words & 0xF
        nib[..., 1::2] = words >> 4
        vals = E2M1[nib]
    vals = vals * np.repeat(np.exp2(scales.astype(np.float64) - 127.0), 8, axis=1)[..., None]
    return vals.transpose(0, 1, 3, 2).reshape(g * 512, n)
def pack4(w):
    words, scales = pack_weight(w, "e2m1")
    return words.reshape(words.shape[0], 128, -1), scales


def unpack4(words, scales):
    return unpack_weight(words.reshape(words.shape[0], 128, -1, 2), scales, "e2m1")


L, R, M = 2048, 1024, 1024


def setup_inputs():
    s, t = mx_kscale(L), mx_kscale(R)
    y = np.random.standard_normal((L, M))
    e = bf(1 + 0.1 * np.random.standard_normal(M))
    w = np.random.standard_normal((L, R)) / np.sqrt(L)
    w_words, w_scales = pack4(w * s[:, None])
    y_words, y_scales = pack4(y / s[:, None])
    return {"w_words": w_words, "w_scales": w_scales,
            "y_words": y_words, "y_scales": y_scales,
            "d": bf((1 + 0.1 * np.random.standard_normal(R)) * t),
            "e": e,
            "vt": bf(np.random.standard_normal((R, L)) / np.sqrt(R) / t[:, None]),
            "x": bf(y * f64(e))}


def reference(w_words, w_scales, y_words, y_scales, d, e, vt, x):
    w = unpack4(w_words, w_scales)
    y = unpack4(y_words, y_scales)
    c = w.T @ y
    c = c * f64(d)[:, None] * f64(e)[None, :]
    v = mxq(f64(vt), 0, "e4m3")
    along = v.T @ mxq(c, 0, "e4m3")
    return f64(x) - along

@@ -1,0 +1,253 @@
+from contextlib import ExitStack
+
+import concourse.mybir as mybir
+from concourse.masks import make_identity
+
+L, R, M = 2048, 1024, 1024
+FLOPS = 2 * L * R * M * 2
+
+F32 = mybir.dt.float32
+BF16 = mybir.dt.bfloat16
+I32 = mybir.dt.int32
+U32 = mybir.dt.uint32
+U8 = mybir.dt.uint8
+FP8X4 = mybir.dt.float8_e4m3fn_x4
+FP4X4 = mybir.dt.float4_e2m1fn_x4
+ALU = mybir.AluOpType
+
+P = 128
+N = 512
+VW = 256
+HELPED = ()
+
+
+def tile_oblique_block_deflation_s4_kernel(tc, w_words, w_scales, y_words, y_scales, d, e, vt, x, out):
+    nc = tc.nc
+    with ExitStack() as ctx:
+        keep = ctx.enter_context(tc.tile_pool(name="keep", bufs=1))
+        ring = ctx.enter_context(tc.tile_pool(name="ring", bufs=2))
+        psum = ctx.enter_context(tc.psum_pool(name="psum", bufs=8))
+        ctx.enter_context(tc.manual_schedule())
+
+        def load_words(src, name, half, g0, g1):
+            t = keep.tile([P, (g1 - g0) * 1024], U8, name=name, align_bytes=64)
+            nc.sync.dma_start(
+                out=t[:].bitcast(I32).rearrange("p (g n) -> p g n", g=g1 - g0),
+                in_=src[g0:g1, :, half * 1024 : (half + 1) * 1024].bitcast(I32).rearrange("g p n -> p g n"),
+            )
+            return t
+
+        def load_scales(queue, plane, src, r):
+            queue.dma_start(
+                out=plane[r:P:32, :].bitcast(I32).rearrange("p (g n) -> p g n", g=4),
+                in_=src[:, r:16:4, :].bitcast(I32).rearrange("g q n -> q g n"),
+            )
+
+        ws_raw = keep.tile([P, 4096], U8, name="ws_raw", align_bytes=64)
+        ys = keep.tile([P, 4096], U8, name="ys", align_bytes=64)
+        nc.vector.memset(ws_raw[:].bitcast(I32), 0)
+        nc.vector.memset(ys[:].bitcast(I32), 0)
+
+        e_rows = keep.tile([P, 8], BF16, name="e_rows")
+        nc.gpsimd.dma_start(out=e_rows[:], in_=e.rearrange("(p j) -> p j", j=8))
+
+        w_raw = {}
+        y_parts = {}
+        w_raw[0, 0] = load_words(w_words, "w_raw00", 0, 0, 2)
+        y_parts[0, 0] = load_words(y_words, "y00", 0, 0, 2)
+        for r in range(4):
+            load_scales(nc.sync, ws_raw, w_scales, r)
+        for r in range(4):
+            load_scales(nc.sync, ys, y_scales, r)
+        w_raw[0, 2] = load_words(w_words, "w_raw02", 0, 2, 4)
+        y_parts[0, 2] = load_words(y_words, "y02", 0, 2, 4)
+        w_raw[1, 0] = load_words(w_words, "w_raw10", 1, 0, 4)
+
+        ident = keep.tile([P, P], F32, name="ident")
+        make_identity(nc, ident[:])
+        d_runs = keep.tile([P, 2, 16], BF16, name="d_runs")
+        d_view = d.rearrange("(g u j) -> u g j", g=2, j=16)
+        for s in range(4):
+            nc.sync.dma_start(out=d_runs[s:P:4, :, 0:13], in_=d_view[:, :, s : s + 13])
+
+        vt_view = vt.rearrange("(g u t s) l -> g s u t l", g=2, t=4, s=4)
+        v_raw = {}
+
+        def load_vt(g, lh):
+            t = keep.tile([P, 4, 1024], BF16, name="v_raw%d%d" % (g, lh))
+            for s in range(4):
+                nc.sync.dma_start(out=t[s:P:4, :, :], in_=vt_view[g, s][:, :, lh * 1024 : (lh + 1) * 1024])
+            v_raw[g, lh] = t
+
+        load_vt(0, 0)
+        load_vt(1, 0)
+        y_parts[1, 0] = load_words(y_words, "y10", 1, 0, 4)
+        load_vt(0, 1)
+        load_vt(1, 1)
+        x_sb = []
+        for c in range(4):
+            t = keep.tile([P, 4, M], BF16, name="x%d" % c)
+            nc.sync.dma_start(out=t[:], in_=x[c * 512 : (c + 1) * 512, :].rearrange("(j p) m -> p j m", p=P))
+            x_sb.append(t)
+
+        e_ps = psum.tile([P, N], F32, tag="acc", name="e_ps")
+        for w in range(4):
+            nc.tensor.transpose(
+                e_ps[:, w * P : (w + 1) * P], e_rows[:].bitcast(F32)[:, w : w + 1].to_broadcast([P, P]), ident[:]
+            )
+        e_all = keep.tile([P, M], BF16, name="e_all")
+        nc.scalar.copy(
+            out=e_all[:].bitcast(F32).rearrange("p (n w) -> p n w", w=4),
+            in_=e_ps[:].rearrange("p (w n) -> p n w", w=4),
+        )
+
+        w_cols = {}
+        ws_cols = {}
+
+        def sort_words(half, g0, g1):
+            t = keep.tile([P, (g1 - g0) * 1024], U8, name="w_cols%d%d" % (half, g0), align_bytes=64)
+            nc.vector.tensor_copy(
+                out=t[:].bitcast(I32).rearrange("p (g t u w) -> p g t u w", t=4, u=32, w=2),
+                in_=w_raw[half, g0][:].bitcast(I32).rearrange("p (g u t w) -> p g t u w", t=4, u=32, w=2),
+            )
+            for g in range(g0, g1):
+                w_cols[half, g] = t[:, (g - g0) * 1024 : (g - g0 + 1) * 1024]
+
+        def sort_scales(half):
+            t = keep.tile([P, 2048], U8, name="ws_cols%d" % half, align_bytes=64)
+            nc.vector.tensor_copy(
+                out=t[:].bitcast(I32).rearrange("p (g t u) -> p g t u", t=4, u=32),
+                in_=ws_raw[:].bitcast(I32).rearrange("p (g h u t) -> p h g t u", h=2, t=4, u=32)[:, half],
+            )
+            ws_cols[half] = t
+
+        y_cols = {}
+        for half, g0, g1 in ((0, 0, 2), (0, 2, 4), (1, 0, 4)):
+            for g in range(g0, g1):
+                y_cols[half, g] = y_parts[half, g0][:, (g - g0) * 1024 : (g - g0 + 1) * 1024]
+
+        sort_words(0, 0, 2)
+        sort_scales(0)
+        sort_words(0, 2, 4)
+
+        h_rows = {}
+        grouped = {}
+        v_mx = {}
+        h_mx = {}
+
+        def interleave(copy, dst, src):
+            copy(
+                out=dst.rearrange("p (c i t) -> p c t i", i=4, t=4),
+                in_=src.rearrange("p t (c i) -> p c t i", i=4),
+            )
+
+        def interleave_v(copy, g, j):
+            t = ring.tile([P, 4 * VW], BF16, tag="v_grouped", name="v_grouped", bufs=6, align_bytes=64)
+            c0 = (j % 4) * VW
+            interleave(copy, t[:], v_raw[g, j // 4][:, :, c0 : c0 + VW])
+            grouped["v", g, j] = t
+
+        def interleave_h(mh, g):
+            t = ring.tile([P, 4 * N], BF16, tag="h_grouped", name="h_grouped", align_bytes=64)
+            interleave(nc.scalar.copy, t[:], h_rows[mh, g][:])
+            grouped["h", mh, g] = t
+
+        def quantise(key):
+            width = VW if key[0] == "v" else N
+            codes = keep.tile([P, width], U32, name="codes_%s%d%d" % key, align_bytes=64)
+            scales = keep.tile([P, width], U8, name="scales_%s%d%d" % key, align_bytes=64)
+            nc.vector.quantize_mx(out=codes[:].bitcast(FP8X4), scales=scales[:], in_=grouped[key][:])
+            (v_mx if key[0] == "v" else h_mx)[key[1], key[2]] = (codes, scales)
+
+        def stage1(mh, g2, t):
+            acc = psum.tile([P, N], F32, tag="acc", name="acc")
+            for g in range(4):
+                nc.tensor.matmul_mx(
+                    out=acc[:],
+                    lhsT=w_cols[g2, g][:, t * 256 : (t + 1) * 256].bitcast(FP4X4),
+                    lhsT_scale=ws_cols[g2][:, (g * 4 + t) * P : (g * 4 + t + 1) * P],
+                    rhs=y_cols[mh, g].bitcast(FP4X4),
+                    rhs_scale=ys[:, g * 1024 + mh * N : g * 1024 + (mh + 1) * N],
+                    start=(g == 0),
+                    stop=(g == 3),
+                )
+            return acc
+
+        def scale_out(mh, g2, t, acc):
+            if t == 0:
+                h_rows[mh, g2] = ring.tile([P, 4, N], BF16, tag="h_rows", name="h_rows")
+            nc.vector.scalar_tensor_tensor(
+                out=h_rows[mh, g2][:, t, :],
+                in0=acc[:],
+                scalar=d_runs[:, g2, 4 * t : 4 * t + 1],
+                in1=e_all[:, mh * N : (mh + 1) * N],
+                op0=ALU.mult,
+                op1=ALU.mult,
+            )
+
+        def stage2(lt, mh):
+            acc = psum.tile([P, N], F32, tag="acc", name="acc")
+            c0 = (lt % 2) * P
+            for g2 in range(2):
+                vc, vs = v_mx[g2, lt // 2]
+                hc, hs = h_mx[mh, g2]
+                nc.tensor.matmul_mx(
+                    out=acc[:],
+                    lhsT=vc[:, c0 : c0 + P].bitcast(FP8X4),
+                    lhsT_scale=vs[:, c0 : c0 + P],
+                    rhs=hc[:].bitcast(FP8X4),
+                    rhs_scale=hs[:],
+                    start=(g2 == 0),
+                    stop=(g2 == 1),
+                )
+            return acc
+
+        def subtract(res, lt, mh, acc):
+            xs = x_sb[lt // 4][:, lt % 4, mh * N : (mh + 1) * N]
+            if mh == 1 and lt in HELPED:
+                tmp = ring.tile([P, N], F32, tag="tmp", name="tmp", bufs=3)
+                nc.scalar.copy(out=tmp[:], in_=acc[:])
+                nc.gpsimd.tensor_tensor(out=res, in0=xs, in1=tmp[:], op=ALU.subtract)
+            else:
+                nc.vector.tensor_tensor(out=res, in0=xs, in1=acc[:], op=ALU.subtract)
+
+        def stage2_pair(pair, mh):
+            accs = [stage2(2 * pair + j, mh) for j in range(2)]
+            res = ring.tile([P, 2, N], F32, tag="res", name="res", bufs=8)
+            dst = out[pair * 2 * P : (pair + 1) * 2 * P, mh * N : (mh + 1) * N].rearrange("(j p) m -> p j m", p=P)
+            last = pair == 7 and mh == 1
+            for j in range(2):
+                subtract(res[:, j, :], 2 * pair + j, mh, accs[j])
+                if last:
+                    nc.sync.dma_start(out=dst[:, j, :], in_=res[:, j, :])
+            if not last:
+                nc.sync.dma_start(out=dst, in_=res[:])
+
+        scalar_v = {2: [(0, 0)], 3: [(0, 1)], 6: [(1, 0)], 7: [(1, 1)], 10: [(0, 4)], 11: [(1, 4)],
+                    13: [(0, 5), (1, 5)], 14: [(0, 6), (1, 6)], 15: [(0, 7), (1, 7)]}
+        vector_v = {2: [(0, 2)], 3: [(0, 3)], 6: [(1, 2)], 7: [(1, 3)]}
+        due = {}
+        for step in range(28):
+            acc = None
+            if step < 16:
+                mh, g2, t = step // 8, (step // 4) % 2, step % 4
+                acc = stage1(mh, g2, t)
+            if step == 1:
+                sort_scales(1)
+                sort_words(1, 0, 4)
+            for key in due.get(step, []):
+                quantise(key)
+            if step in (4, 8, 12, 16):
+                hm, hg = (step - 4) // 8, ((step - 4) // 4) % 2
+                interleave_h(hm, hg)
+                due.setdefault(step + (3 if step == 16 else 2), []).append(("h", hm, hg))
+            for g, j in scalar_v.get(step, []):
+                interleave_v(nc.scalar.copy, g, j)
+                due.setdefault(step + 2, []).append(("v", g, j))
+            for g, j in vector_v.get(step, []):
+                interleave_v(nc.vector.tensor_copy, g, j)
+                due.setdefault(step + 2, []).append(("v", g, j))
+            if acc is not None:
+                scale_out(mh, g2, t, acc)
+            if step >= 12:
+                stage2_pair((step - 12) % 8, (step - 12) // 8)

@@ -19,6 +19,15 @@ P = 128
 N = 512
 VW = 256
 HELPED = ()
+FIRST = 13
+PERM = 3
+HLAG = (3,3,3,2)
+NF = 6
+ELAG = 0
+EEND = 16
+SCALAR_V = {2: [(0, 0)], 3: [(0, 1)], 6: [(1, 0)], 7: [(1, 1)], 10: [(0, 4)], 13: [(1, 4)], 14: [(0, 5), (1, 5)],
+            17: [(0, 6)], 18: [(1, 6)], 19: [(0, 7)], 20: [(1, 7)]}
+VECTOR_V = {2: [(0, 2)], 4: [(0, 3)], 8: [(1, 2)], 9: [(1, 3)]}
 
 
 def tile_oblique_block_deflation_s4_kernel(tc, w_words, w_scales, y_words, y_scales, d, e, vt, x, out):
@@ -37,16 +46,20 @@ def tile_oblique_block_deflation_s4_kernel(tc, w_words, w_scales, y_words, y_sca
             )
             return t
 
-        def load_scales(queue, plane, src, r):
-            queue.dma_start(
-                out=plane[r:P:32, :].bitcast(I32).rearrange("p (g n) -> p g n", g=4),
-                in_=src[:, r:16:4, :].bitcast(I32).rearrange("g q n -> q g n"),
-            )
+        def load_scales(plane, src, half):
+            for r in range(4):
+                nc.sync.dma_start(
+                    out=plane[r:P:32, :].bitcast(I32).rearrange("p (g n) -> p g n", g=4),
+                    in_=src[:, r:16:4, half * N : (half + 1) * N].bitcast(I32).rearrange("g q n -> q g n"),
+                )
 
-        ws_raw = keep.tile([P, 4096], U8, name="ws_raw", align_bytes=64)
-        ys = keep.tile([P, 4096], U8, name="ys", align_bytes=64)
-        nc.vector.memset(ws_raw[:].bitcast(I32), 0)
-        nc.vector.memset(ys[:].bitcast(I32), 0)
+        ws_raw = []
+        ys = []
+        for half in range(2):
+            for planes, name in ((ws_raw, "ws_raw%d"), (ys, "ys%d")):
+                t = keep.tile([P, 4 * N], U8, name=name % half, align_bytes=64)
+                nc.vector.memset(t[:].bitcast(I32), 0)
+                planes.append(t)
 
         e_rows = keep.tile([P, 8], BF16, name="e_rows")
         nc.gpsimd.dma_start(out=e_rows[:], in_=e.rearrange("(p j) -> p j", j=8))
@@ -55,40 +68,46 @@ def tile_oblique_block_deflation_s4_kernel(tc, w_words, w_scales, y_words, y_sca
         y_parts = {}
         w_raw[0, 0] = load_words(w_words, "w_raw00", 0, 0, 2)
         y_parts[0, 0] = load_words(y_words, "y00", 0, 0, 2)
-        for r in range(4):
-            load_scales(nc.sync, ws_raw, w_scales, r)
-        for r in range(4):
-            load_scales(nc.sync, ys, y_scales, r)
+        load_scales(ws_raw[0], w_scales, 0)
+        load_scales(ys[0], y_scales, 0)
         w_raw[0, 2] = load_words(w_words, "w_raw02", 0, 2, 4)
         y_parts[0, 2] = load_words(y_words, "y02", 0, 2, 4)
-        w_raw[1, 0] = load_words(w_words, "w_raw10", 1, 0, 4)
-
-        ident = keep.tile([P, P], F32, name="ident")
-        make_identity(nc, ident[:])
         d_runs = keep.tile([P, 2, 16], BF16, name="d_runs")
         d_view = d.rearrange("(g u j) -> u g j", g=2, j=16)
         for s in range(4):
             nc.sync.dma_start(out=d_runs[s:P:4, :, 0:13], in_=d_view[:, :, s : s + 13])
 
-        vt_view = vt.rearrange("(g u t s) l -> g s u t l", g=2, t=4, s=4)
+        ident = keep.tile([P, P], F32, name="ident")
+        make_identity(nc, ident[:])
+
+        vt_view = vt.rearrange("(g u t s) l -> g t u s l", g=2, t=4, s=4)
         v_raw = {}
 
         def load_vt(g, lh):
             t = keep.tile([P, 4, 1024], BF16, name="v_raw%d%d" % (g, lh))
             for s in range(4):
-                nc.sync.dma_start(out=t[s:P:4, :, :], in_=vt_view[g, s][:, :, lh * 1024 : (lh + 1) * 1024])
+                nc.sync.dma_start(out=t[:, s, :], in_=vt_view[g, s][:, :, lh * 1024 : (lh + 1) * 1024])
             v_raw[g, lh] = t
 
-        load_vt(0, 0)
-        load_vt(1, 0)
-        y_parts[1, 0] = load_words(y_words, "y10", 1, 0, 4)
-        load_vt(0, 1)
-        load_vt(1, 1)
-        x_sb = []
-        for c in range(4):
+        x_sb = {}
+
+        def load_x(c):
             t = keep.tile([P, 4, M], BF16, name="x%d" % c)
             nc.sync.dma_start(out=t[:], in_=x[c * 512 : (c + 1) * 512, :].rearrange("(j p) m -> p j m", p=P))
-            x_sb.append(t)
+            x_sb[c] = t
+
+        load_vt(0, 0)
+        load_scales(ws_raw[1], w_scales, 1)
+        w_raw[1, 0] = load_words(w_words, "w_raw10", 1, 0, 2)
+        w_raw[1, 2] = load_words(w_words, "w_raw12", 1, 2, 4)
+        load_scales(ys[1], y_scales, 1)
+        y_parts[1, 0] = load_words(y_words, "y10", 1, 0, 4)
+        load_vt(1, 0)
+        load_vt(0, 1)
+        load_x(0)
+        load_vt(1, 1)
+        for c in range(1, 4):
+            load_x(c)
 
         e_ps = psum.tile([P, N], F32, tag="acc", name="e_ps")
         for w in range(4):
@@ -117,7 +136,7 @@ def tile_oblique_block_deflation_s4_kernel(tc, w_words, w_scales, y_words, y_sca
             t = keep.tile([P, 2048], U8, name="ws_cols%d" % half, align_bytes=64)
             nc.vector.tensor_copy(
                 out=t[:].bitcast(I32).rearrange("p (g t u) -> p g t u", t=4, u=32),
-                in_=ws_raw[:].bitcast(I32).rearrange("p (g h u t) -> p h g t u", h=2, t=4, u=32)[:, half],
+                in_=ws_raw[half][:].bitcast(I32).rearrange("p (g u t) -> p g t u", t=4, u=32),
             )
             ws_cols[half] = t
 
@@ -167,7 +186,7 @@ def tile_oblique_block_deflation_s4_kernel(tc, w_words, w_scales, y_words, y_sca
                     lhsT=w_cols[g2, g][:, t * 256 : (t + 1) * 256].bitcast(FP4X4),
                     lhsT_scale=ws_cols[g2][:, (g * 4 + t) * P : (g * 4 + t + 1) * P],
                     rhs=y_cols[mh, g].bitcast(FP4X4),
-                    rhs_scale=ys[:, g * 1024 + mh * N : g * 1024 + (mh + 1) * N],
+                    rhs_scale=ys[mh][:, g * N : (g + 1) * N],
                     start=(g == 0),
                     stop=(g == 3),
                 )
@@ -202,52 +221,56 @@ def tile_oblique_block_deflation_s4_kernel(tc, w_words, w_scales, y_words, y_sca
                 )
             return acc
 
-        def subtract(res, lt, mh, acc):
+        def subtract(res, lt, mh, acc, helped):
             xs = x_sb[lt // 4][:, lt % 4, mh * N : (mh + 1) * N]
-            if mh == 1 and lt in HELPED:
+            if helped:
                 tmp = ring.tile([P, N], F32, tag="tmp", name="tmp", bufs=3)
                 nc.scalar.copy(out=tmp[:], in_=acc[:])
                 nc.gpsimd.tensor_tensor(out=res, in0=xs, in1=tmp[:], op=ALU.subtract)
             else:
                 nc.vector.tensor_tensor(out=res, in0=xs, in1=acc[:], op=ALU.subtract)
 
-        def stage2_pair(pair, mh):
-            accs = [stage2(2 * pair + j, mh) for j in range(2)]
+        def finish_pair(pair, mh, helped, accs):
             res = ring.tile([P, 2, N], F32, tag="res", name="res", bufs=8)
             dst = out[pair * 2 * P : (pair + 1) * 2 * P, mh * N : (mh + 1) * N].rearrange("(j p) m -> p j m", p=P)
             last = pair == 7 and mh == 1
             for j in range(2):
-                subtract(res[:, j, :], 2 * pair + j, mh, accs[j])
+                subtract(res[:, j, :], 2 * pair + j, mh, accs[j], helped and j == 0)
                 if last:
                     nc.sync.dma_start(out=dst[:, j, :], in_=res[:, j, :])
             if not last:
                 nc.sync.dma_start(out=dst, in_=res[:])
 
-        scalar_v = {2: [(0, 0)], 3: [(0, 1)], 6: [(1, 0)], 7: [(1, 1)], 10: [(0, 4)], 11: [(1, 4)],
-                    13: [(0, 5), (1, 5)], 14: [(0, 6), (1, 6)], 15: [(0, 7), (1, 7)]}
-        vector_v = {2: [(0, 2)], 3: [(0, 3)], 6: [(1, 2)], 7: [(1, 3)]}
+        scalar_v = SCALAR_V
+        vector_v = VECTOR_V
+        pairs = [(p, 0) for p in range(NF)] + [(p, 1) for p in range(NF)] + [(p, h) for p in range(NF, 8) for h in range(2)]
         due = {}
-        for step in range(28):
+        waiting = []
+        for step in range(FIRST + 16):
             acc = None
             if step < 16:
                 mh, g2, t = step // 8, (step // 4) % 2, step % 4
                 acc = stage1(mh, g2, t)
-            if step == 1:
+            if step == PERM:
                 sort_scales(1)
-                sort_words(1, 0, 4)
+                sort_words(1, 0, 2)
+                sort_words(1, 2, 4)
             for key in due.get(step, []):
                 quantise(key)
             if step in (4, 8, 12, 16):
                 hm, hg = (step - 4) // 8, ((step - 4) // 4) % 2
                 interleave_h(hm, hg)
-                due.setdefault(step + (3 if step == 16 else 2), []).append(("h", hm, hg))
+                due.setdefault(step + HLAG[step // 4 - 1], []).append(("h", hm, hg))
             for g, j in scalar_v.get(step, []):
                 interleave_v(nc.scalar.copy, g, j)
                 due.setdefault(step + 2, []).append(("v", g, j))
             for g, j in vector_v.get(step, []):
                 interleave_v(nc.vector.tensor_copy, g, j)
-                due.setdefault(step + 2, []).append(("v", g, j))
+                due.setdefault(step + 1, []).append(("v", g, j))
             if acc is not None:
                 scale_out(mh, g2, t, acc)
-            if step >= 12:
-                stage2_pair((step - 12) % 8, (step - 12) // 8)
+            if FIRST <= step < FIRST + 16:
+                pair, ph = pairs[step - FIRST]
+                waiting.append((pair, ph, step in HELPED, [stage2(2 * pair + j, ph) for j in range(2)]))
+            while len(waiting) > (ELAG if step < EEND else 0):
+                finish_pair(*waiting.pop(0))

@@ -17,17 +17,15 @@ ALU = mybir.AluOpType
 
 P = 128
 N = 512
-VW = 256
+VW = 512
 HELPED = ()
-FIRST = 13
-PERM = 3
-HLAG = (3,3,3,2)
-NF = 6
-ELAG = 0
-EEND = 16
-SCALAR_V = {2: [(0, 0)], 3: [(0, 1)], 6: [(1, 0)], 7: [(1, 1)], 10: [(0, 4)], 13: [(1, 4)], 14: [(0, 5), (1, 5)],
-            17: [(0, 6)], 18: [(1, 6)], 19: [(0, 7)], 20: [(1, 7)]}
-VECTOR_V = {2: [(0, 2)], 4: [(0, 3)], 8: [(1, 2)], 9: [(1, 3)]}
+EARLY = 0
+QUAD = 0
+REV = 2
+RB = 14
+PB = 0
+PJ = 1
+QB = 3
 
 
 def tile_oblique_block_deflation_s4_kernel(tc, w_words, w_scales, y_words, y_scales, d, e, vt, x, out):
@@ -64,12 +62,26 @@ def tile_oblique_block_deflation_s4_kernel(tc, w_words, w_scales, y_words, y_sca
         e_rows = keep.tile([P, 8], BF16, name="e_rows")
         nc.gpsimd.dma_start(out=e_rows[:], in_=e.rearrange("(p j) -> p j", j=8))
 
+        vt_view = vt.rearrange("(g u t s) l -> g t u s l", g=2, t=4, s=4)
+        v_raw = {}
+
+        def load_vt(g, j0, j1):
+            t = keep.tile([P, 4, (j1 - j0) * VW], BF16, name="v_raw%d%d" % (g, j0))
+            for s in range(4):
+                nc.sync.dma_start(out=t[:, s, :], in_=vt_view[g, s][:, :, j0 * VW : j1 * VW])
+            for j in range(j0, j1):
+                v_raw[g, j] = t[:, :, (j - j0) * VW : (j - j0 + 1) * VW]
+
         w_raw = {}
         y_parts = {}
+        if EARLY == 2:
+            load_vt(0, 0, 1)
         w_raw[0, 0] = load_words(w_words, "w_raw00", 0, 0, 2)
         y_parts[0, 0] = load_words(y_words, "y00", 0, 0, 2)
         load_scales(ws_raw[0], w_scales, 0)
         load_scales(ys[0], y_scales, 0)
+        if EARLY == 1:
+            load_vt(0, 0, 1)
         w_raw[0, 2] = load_words(w_words, "w_raw02", 0, 2, 4)
         y_parts[0, 2] = load_words(y_words, "y02", 0, 2, 4)
         d_runs = keep.tile([P, 2, 16], BF16, name="d_runs")
@@ -80,15 +92,6 @@ def tile_oblique_block_deflation_s4_kernel(tc, w_words, w_scales, y_words, y_sca
         ident = keep.tile([P, P], F32, name="ident")
         make_identity(nc, ident[:])
 
-        vt_view = vt.rearrange("(g u t s) l -> g t u s l", g=2, t=4, s=4)
-        v_raw = {}
-
-        def load_vt(g, lh):
-            t = keep.tile([P, 4, 1024], BF16, name="v_raw%d%d" % (g, lh))
-            for s in range(4):
-                nc.sync.dma_start(out=t[:, s, :], in_=vt_view[g, s][:, :, lh * 1024 : (lh + 1) * 1024])
-            v_raw[g, lh] = t
-
         x_sb = {}
 
         def load_x(c):
@@ -96,16 +99,15 @@ def tile_oblique_block_deflation_s4_kernel(tc, w_words, w_scales, y_words, y_sca
             nc.sync.dma_start(out=t[:], in_=x[c * 512 : (c + 1) * 512, :].rearrange("(j p) m -> p j m", p=P))
             x_sb[c] = t
 
-        load_vt(0, 0)
         load_scales(ws_raw[1], w_scales, 1)
-        w_raw[1, 0] = load_words(w_words, "w_raw10", 1, 0, 2)
-        w_raw[1, 2] = load_words(w_words, "w_raw12", 1, 2, 4)
+        w_raw[1, 0] = load_words(w_words, "w_raw10", 1, 0, 4)
+        load_vt(0, 1 if EARLY else 0, 2)
         load_scales(ys[1], y_scales, 1)
         y_parts[1, 0] = load_words(y_words, "y10", 1, 0, 4)
-        load_vt(1, 0)
-        load_vt(0, 1)
+        load_vt(1, 0, 2)
+        load_vt(0, 2, 4)
         load_x(0)
-        load_vt(1, 1)
+        load_vt(1, 2, 4)
         for c in range(1, 4):
             load_x(c)
 
@@ -150,6 +152,7 @@ def tile_oblique_block_deflation_s4_kernel(tc, w_words, w_scales, y_words, y_sca
         sort_words(0, 2, 4)
 
         h_rows = {}
+        stores = {}
         grouped = {}
         v_mx = {}
         h_mx = {}
@@ -161,9 +164,8 @@ def tile_oblique_block_deflation_s4_kernel(tc, w_words, w_scales, y_words, y_sca
             )
 
         def interleave_v(copy, g, j):
-            t = ring.tile([P, 4 * VW], BF16, tag="v_grouped", name="v_grouped", bufs=6, align_bytes=64)
-            c0 = (j % 4) * VW
-            interleave(copy, t[:], v_raw[g, j // 4][:, :, c0 : c0 + VW])
+            t = ring.tile([P, 4 * VW], BF16, tag="v_grouped", name="v_grouped", bufs=3, align_bytes=64)
+            interleave(copy, t[:], v_raw[g, j])
             grouped["v", g, j] = t
 
         def interleave_h(mh, g):
@@ -193,8 +195,6 @@ def tile_oblique_block_deflation_s4_kernel(tc, w_words, w_scales, y_words, y_sca
             return acc
 
         def scale_out(mh, g2, t, acc):
-            if t == 0:
-                h_rows[mh, g2] = ring.tile([P, 4, N], BF16, tag="h_rows", name="h_rows")
             nc.vector.scalar_tensor_tensor(
                 out=h_rows[mh, g2][:, t, :],
                 in0=acc[:],
@@ -206,9 +206,9 @@ def tile_oblique_block_deflation_s4_kernel(tc, w_words, w_scales, y_words, y_sca
 
         def stage2(lt, mh):
             acc = psum.tile([P, N], F32, tag="acc", name="acc")
-            c0 = (lt % 2) * P
+            c0 = (lt % 4) * P
             for g2 in range(2):
-                vc, vs = v_mx[g2, lt // 2]
+                vc, vs = v_mx[g2, lt // 4]
                 hc, hs = h_mx[mh, g2]
                 nc.tensor.matmul_mx(
                     out=acc[:],
@@ -221,56 +221,56 @@ def tile_oblique_block_deflation_s4_kernel(tc, w_words, w_scales, y_words, y_sca
                 )
             return acc
 
-        def subtract(res, lt, mh, acc, helped):
+        def subtract(res, lt, mh, acc):
             xs = x_sb[lt // 4][:, lt % 4, mh * N : (mh + 1) * N]
-            if helped:
-                tmp = ring.tile([P, N], F32, tag="tmp", name="tmp", bufs=3)
-                nc.scalar.copy(out=tmp[:], in_=acc[:])
-                nc.gpsimd.tensor_tensor(out=res, in0=xs, in1=tmp[:], op=ALU.subtract)
-            else:
-                nc.vector.tensor_tensor(out=res, in0=xs, in1=acc[:], op=ALU.subtract)
+            nc.vector.tensor_tensor(out=res, in0=xs, in1=acc[:], op=ALU.subtract)
 
-        def finish_pair(pair, mh, helped, accs):
-            res = ring.tile([P, 2, N], F32, tag="res", name="res", bufs=8)
+        def finish_pair(pair, mh, accs):
+            res = ring.tile([P, 2, N], F32, tag="res", name="res", bufs=RB)
             dst = out[pair * 2 * P : (pair + 1) * 2 * P, mh * N : (mh + 1) * N].rearrange("(j p) m -> p j m", p=P)
             last = pair == 7 and mh == 1
-            for j in range(2):
-                subtract(res[:, j, :], 2 * pair + j, mh, accs[j], helped and j == 0)
+            for j in (range(2) if last else (1, 0)):
+                subtract(res[:, j, :], 2 * pair + j, mh, accs[j])
                 if last:
                     nc.sync.dma_start(out=dst[:, j, :], in_=res[:, j, :])
             if not last:
                 nc.sync.dma_start(out=dst, in_=res[:])
 
-        scalar_v = SCALAR_V
-        vector_v = VECTOR_V
-        pairs = [(p, 0) for p in range(NF)] + [(p, 1) for p in range(NF)] + [(p, h) for p in range(NF, 8) for h in range(2)]
-        due = {}
-        waiting = []
-        for step in range(FIRST + 16):
-            acc = None
-            if step < 16:
-                mh, g2, t = step // 8, (step // 4) % 2, step % 4
-                acc = stage1(mh, g2, t)
-            if step == PERM:
-                sort_scales(1)
-                sort_words(1, 0, 2)
-                sort_words(1, 2, 4)
-            for key in due.get(step, []):
-                quantise(key)
-            if step in (4, 8, 12, 16):
-                hm, hg = (step - 4) // 8, ((step - 4) // 4) % 2
-                interleave_h(hm, hg)
-                due.setdefault(step + HLAG[step // 4 - 1], []).append(("h", hm, hg))
-            for g, j in scalar_v.get(step, []):
-                interleave_v(nc.scalar.copy, g, j)
-                due.setdefault(step + 2, []).append(("v", g, j))
-            for g, j in vector_v.get(step, []):
-                interleave_v(nc.vector.tensor_copy, g, j)
-                due.setdefault(step + 1, []).append(("v", g, j))
-            if acc is not None:
-                scale_out(mh, g2, t, acc)
-            if FIRST <= step < FIRST + 16:
-                pair, ph = pairs[step - FIRST]
-                waiting.append((pair, ph, step in HELPED, [stage2(2 * pair + j, ph) for j in range(2)]))
-            while len(waiting) > (ELAG if step < EEND else 0):
-                finish_pair(*waiting.pop(0))
+        pieces = [("v", 0, 0), ("v", 0, 1), ("h", 0, 0), ("v", 1, 0), ("h", 0, 1), ("v", 1, 1), ("h", 1, 0), ("h", 1, 1)]
+        pieces += [("v", g, j) for j in (2, 3) for g in range(2)]
+        pairs = [(p, 0) for p in range(4)] + [(p, 1) for p in range(4)] + [(p, h) for p in range(4, 8) for h in range(2)]
+        if EARLY:
+            interleave_v(nc.vector.tensor_copy, 0, 0)
+        for beat in range(16):
+            if beat < 8:
+                mh, g2, t0 = beat // 4, (beat // 2) % 2, 2 * (beat % 2)
+                accs = [stage1(mh, g2, t0 + j) for j in range(2)]
+            if beat == QB:
+                quantise(pieces[0])
+            if 3 <= beat < len(pieces) + 2:
+                quantise(pieces[beat - 2])
+            if beat < 8:
+                if t0 == 0:
+                    h_rows[mh, g2] = ring.tile([P, 4, N], BF16, tag="h_rows", name="h_rows", bufs=4)
+                for j in (range(2) if beat < REV else (1, 0)):
+                    scale_out(mh, g2, t0 + j, accs[j])
+                    if beat == PB and j == PJ:
+                        sort_scales(1)
+                        sort_words(1, 0, 4)
+            else:
+                both = pairs[2 * beat - 16 : 2 * beat - 14]
+                if QUAD and beat < 14:
+                    accs = [[stage2(2 * p + j, h) for j in range(2)] for p, h in both]
+                    for n in (1, 0):
+                        finish_pair(both[n][0], both[n][1], accs[n])
+                else:
+                    for p, h in both:
+                        finish_pair(p, h, [stage2(2 * p + j, h) for j in range(2)])
+            if beat == 1:
+                interleave_v(nc.vector.tensor_copy, 0, 0)
+            if 0 < beat < len(pieces):
+                kind, a, b = pieces[beat]
+                if kind == "h":
+                    interleave_h(a, b)
+                else:
+                    interleave_v(nc.vector.tensor_copy if beat in (0, 3) else nc.scalar.copy, a, b)

from contextlib import ExitStack

import concourse.mybir as mybir
from concourse.masks import make_identity

L, R, M = 2048, 1024, 1024
FLOPS = 2 * L * R * M * 2

F32 = mybir.dt.float32
BF16 = mybir.dt.bfloat16
I32 = mybir.dt.int32
U32 = mybir.dt.uint32
U8 = mybir.dt.uint8
FP8X4 = mybir.dt.float8_e4m3fn_x4
FP4X4 = mybir.dt.float4_e2m1fn_x4
ALU = mybir.AluOpType

P = 128
N = 512
VW = 512
HELPED = ()
EARLY = 0
QUAD = 0
REV = 2
RB = 14
PB = 0
PJ = 1
QB = 3


def tile_oblique_block_deflation_s4_kernel(tc, w_words, w_scales, y_words, y_scales, d, e, vt, x, out):
    nc = tc.nc
    with ExitStack() as ctx:
        keep = ctx.enter_context(tc.tile_pool(name="keep", bufs=1))
        ring = ctx.enter_context(tc.tile_pool(name="ring", bufs=2))
        psum = ctx.enter_context(tc.psum_pool(name="psum", bufs=8))
        ctx.enter_context(tc.manual_schedule())

        def load_words(src, name, half, g0, g1):
            t = keep.tile([P, (g1 - g0) * 1024], U8, name=name, align_bytes=64)
            nc.sync.dma_start(
                out=t[:].bitcast(I32).rearrange("p (g n) -> p g n", g=g1 - g0),
                in_=src[g0:g1, :, half * 1024 : (half + 1) * 1024].bitcast(I32).rearrange("g p n -> p g n"),
            )
            return t

        def load_scales(plane, src, half):
            for r in range(4):
                nc.sync.dma_start(
                    out=plane[r:P:32, :].bitcast(I32).rearrange("p (g n) -> p g n", g=4),
                    in_=src[:, r:16:4, half * N : (half + 1) * N].bitcast(I32).rearrange("g q n -> q g n"),
                )

        ws_raw = []
        ys = []
        for half in range(2):
            for planes, name in ((ws_raw, "ws_raw%d"), (ys, "ys%d")):
                t = keep.tile([P, 4 * N], U8, name=name % half, align_bytes=64)
                nc.vector.memset(t[:].bitcast(I32), 0)
                planes.append(t)

        e_rows = keep.tile([P, 8], BF16, name="e_rows")
        nc.gpsimd.dma_start(out=e_rows[:], in_=e.rearrange("(p j) -> p j", j=8))

        vt_view = vt.rearrange("(g u t s) l -> g t u s l", g=2, t=4, s=4)
        v_raw = {}

        def load_vt(g, j0, j1):
            t = keep.tile([P, 4, (j1 - j0) * VW], BF16, name="v_raw%d%d" % (g, j0))
            for s in range(4):
                nc.sync.dma_start(out=t[:, s, :], in_=vt_view[g, s][:, :, j0 * VW : j1 * VW])
            for j in range(j0, j1):
                v_raw[g, j] = t[:, :, (j - j0) * VW : (j - j0 + 1) * VW]

        w_raw = {}
        y_parts = {}
        if EARLY == 2:
            load_vt(0, 0, 1)
        w_raw[0, 0] = load_words(w_words, "w_raw00", 0, 0, 2)
        y_parts[0, 0] = load_words(y_words, "y00", 0, 0, 2)
        load_scales(ws_raw[0], w_scales, 0)
        load_scales(ys[0], y_scales, 0)
        if EARLY == 1:
            load_vt(0, 0, 1)
        w_raw[0, 2] = load_words(w_words, "w_raw02", 0, 2, 4)
        y_parts[0, 2] = load_words(y_words, "y02", 0, 2, 4)
        d_runs = keep.tile([P, 2, 16], BF16, name="d_runs")
        d_view = d.rearrange("(g u j) -> u g j", g=2, j=16)
        for s in range(4):
            nc.sync.dma_start(out=d_runs[s:P:4, :, 0:13], in_=d_view[:, :, s : s + 13])

        ident = keep.tile([P, P], F32, name="ident")
        make_identity(nc, ident[:])

        x_sb = {}

        def load_x(c):
            t = keep.tile([P, 4, M], BF16, name="x%d" % c)
            nc.sync.dma_start(out=t[:], in_=x[c * 512 : (c + 1) * 512, :].rearrange("(j p) m -> p j m", p=P))
            x_sb[c] = t

        load_scales(ws_raw[1], w_scales, 1)
        w_raw[1, 0] = load_words(w_words, "w_raw10", 1, 0, 4)
        load_vt(0, 1 if EARLY else 0, 2)
        load_scales(ys[1], y_scales, 1)
        y_parts[1, 0] = load_words(y_words, "y10", 1, 0, 4)
        load_vt(1, 0, 2)
        load_vt(0, 2, 4)
        load_x(0)
        load_vt(1, 2, 4)
        for c in range(1, 4):
            load_x(c)

        e_ps = psum.tile([P, N], F32, tag="acc", name="e_ps")
        for w in range(4):
            nc.tensor.transpose(
                e_ps[:, w * P : (w + 1) * P], e_rows[:].bitcast(F32)[:, w : w + 1].to_broadcast([P, P]), ident[:]
            )
        e_all = keep.tile([P, M], BF16, name="e_all")
        nc.scalar.copy(
            out=e_all[:].bitcast(F32).rearrange("p (n w) -> p n w", w=4),
            in_=e_ps[:].rearrange("p (w n) -> p n w", w=4),
        )

        w_cols = {}
        ws_cols = {}

        def sort_words(half, g0, g1):
            t = keep.tile([P, (g1 - g0) * 1024], U8, name="w_cols%d%d" % (half, g0), align_bytes=64)
            nc.vector.tensor_copy(
                out=t[:].bitcast(I32).rearrange("p (g t u w) -> p g t u w", t=4, u=32, w=2),
                in_=w_raw[half, g0][:].bitcast(I32).rearrange("p (g u t w) -> p g t u w", t=4, u=32, w=2),
            )
            for g in range(g0, g1):
                w_cols[half, g] = t[:, (g - g0) * 1024 : (g - g0 + 1) * 1024]

        def sort_scales(half):
            t = keep.tile([P, 2048], U8, name="ws_cols%d" % half, align_bytes=64)
            nc.vector.tensor_copy(
                out=t[:].bitcast(I32).rearrange("p (g t u) -> p g t u", t=4, u=32),
                in_=ws_raw[half][:].bitcast(I32).rearrange("p (g u t) -> p g t u", t=4, u=32),
            )
            ws_cols[half] = t

        y_cols = {}
        for half, g0, g1 in ((0, 0, 2), (0, 2, 4), (1, 0, 4)):
            for g in range(g0, g1):
                y_cols[half, g] = y_parts[half, g0][:, (g - g0) * 1024 : (g - g0 + 1) * 1024]

        sort_words(0, 0, 2)
        sort_scales(0)
        sort_words(0, 2, 4)

        h_rows = {}
        stores = {}
        grouped = {}
        v_mx = {}
        h_mx = {}

        def interleave(copy, dst, src):
            copy(
                out=dst.rearrange("p (c i t) -> p c t i", i=4, t=4),
                in_=src.rearrange("p t (c i) -> p c t i", i=4),
            )

        def interleave_v(copy, g, j):
            t = ring.tile([P, 4 * VW], BF16, tag="v_grouped", name="v_grouped", bufs=3, align_bytes=64)
            interleave(copy, t[:], v_raw[g, j])
            grouped["v", g, j] = t

        def interleave_h(mh, g):
            t = ring.tile([P, 4 * N], BF16, tag="h_grouped", name="h_grouped", align_bytes=64)
            interleave(nc.scalar.copy, t[:], h_rows[mh, g][:])
            grouped["h", mh, g] = t

        def quantise(key):
            width = VW if key[0] == "v" else N
            codes = keep.tile([P, width], U32, name="codes_%s%d%d" % key, align_bytes=64)
            scales = keep.tile([P, width], U8, name="scales_%s%d%d" % key, align_bytes=64)
            nc.vector.quantize_mx(out=codes[:].bitcast(FP8X4), scales=scales[:], in_=grouped[key][:])
            (v_mx if key[0] == "v" else h_mx)[key[1], key[2]] = (codes, scales)

        def stage1(mh, g2, t):
            acc = psum.tile([P, N], F32, tag="acc", name="acc")
            for g in range(4):
                nc.tensor.matmul_mx(
                    out=acc[:],
                    lhsT=w_cols[g2, g][:, t * 256 : (t + 1) * 256].bitcast(FP4X4),
                    lhsT_scale=ws_cols[g2][:, (g * 4 + t) * P : (g * 4 + t + 1) * P],
                    rhs=y_cols[mh, g].bitcast(FP4X4),
                    rhs_scale=ys[mh][:, g * N : (g + 1) * N],
                    start=(g == 0),
                    stop=(g == 3),
                )
            return acc

        def scale_out(mh, g2, t, acc):
            nc.vector.scalar_tensor_tensor(
                out=h_rows[mh, g2][:, t, :],
                in0=acc[:],
                scalar=d_runs[:, g2, 4 * t : 4 * t + 1],
                in1=e_all[:, mh * N : (mh + 1) * N],
                op0=ALU.mult,
                op1=ALU.mult,
            )

        def stage2(lt, mh):
            acc = psum.tile([P, N], F32, tag="acc", name="acc")
            c0 = (lt % 4) * P
            for g2 in range(2):
                vc, vs = v_mx[g2, lt // 4]
                hc, hs = h_mx[mh, g2]
                nc.tensor.matmul_mx(
                    out=acc[:],
                    lhsT=vc[:, c0 : c0 + P].bitcast(FP8X4),
                    lhsT_scale=vs[:, c0 : c0 + P],
                    rhs=hc[:].bitcast(FP8X4),
                    rhs_scale=hs[:],
                    start=(g2 == 0),
                    stop=(g2 == 1),
                )
            return acc

        def subtract(res, lt, mh, acc):
            xs = x_sb[lt // 4][:, lt % 4, mh * N : (mh + 1) * N]
            nc.vector.tensor_tensor(out=res, in0=xs, in1=acc[:], op=ALU.subtract)

        def finish_pair(pair, mh, accs):
            res = ring.tile([P, 2, N], F32, tag="res", name="res", bufs=RB)
            dst = out[pair * 2 * P : (pair + 1) * 2 * P, mh * N : (mh + 1) * N].rearrange("(j p) m -> p j m", p=P)
            last = pair == 7 and mh == 1
            for j in (range(2) if last else (1, 0)):
                subtract(res[:, j, :], 2 * pair + j, mh, accs[j])
                if last:
                    nc.sync.dma_start(out=dst[:, j, :], in_=res[:, j, :])
            if not last:
                nc.sync.dma_start(out=dst, in_=res[:])

        pieces = [("v", 0, 0), ("v", 0, 1), ("h", 0, 0), ("v", 1, 0), ("h", 0, 1), ("v", 1, 1), ("h", 1, 0), ("h", 1, 1)]
        pieces += [("v", g, j) for j in (2, 3) for g in range(2)]
        pairs = [(p, 0) for p in range(4)] + [(p, 1) for p in range(4)] + [(p, h) for p in range(4, 8) for h in range(2)]
        if EARLY:
            interleave_v(nc.vector.tensor_copy, 0, 0)
        for beat in range(16):
            if beat < 8:
                mh, g2, t0 = beat // 4, (beat // 2) % 2, 2 * (beat % 2)
                accs = [stage1(mh, g2, t0 + j) for j in range(2)]
            if beat == QB:
                quantise(pieces[0])
            if 3 <= beat < len(pieces) + 2:
                quantise(pieces[beat - 2])
            if beat < 8:
                if t0 == 0:
                    h_rows[mh, g2] = ring.tile([P, 4, N], BF16, tag="h_rows", name="h_rows", bufs=4)
                for j in (range(2) if beat < REV else (1, 0)):
                    scale_out(mh, g2, t0 + j, accs[j])
                    if beat == PB and j == PJ:
                        sort_scales(1)
                        sort_words(1, 0, 4)
            else:
                both = pairs[2 * beat - 16 : 2 * beat - 14]
                if QUAD and beat < 14:
                    accs = [[stage2(2 * p + j, h) for j in range(2)] for p, h in both]
                    for n in (1, 0):
                        finish_pair(both[n][0], both[n][1], accs[n])
                else:
                    for p, h in both:
                        finish_pair(p, h, [stage2(2 * p + j, h) for j in range(2)])
            if beat == 1:
                interleave_v(nc.vector.tensor_copy, 0, 0)
            if 0 < beat < len(pieces):
                kind, a, b = pieces[beat]
                if kind == "h":
                    interleave_h(a, b)
                else:
                    interleave_v(nc.vector.tensor_copy if beat in (0, 3) else nc.scalar.copy, a, b)
